import numpy as np
import ml_dtypes


def mxq(x, axis, fmt="e4m3"):
    dtype, down = {"e4m3": (ml_dtypes.float8_e4m3fn, 7), "e5m2": (ml_dtypes.float8_e5m2, 14)}[fmt]
    v = np.moveaxis(np.asarray(x, np.float32).astype(ml_dtypes.bfloat16).astype(np.float64), axis, -1)
    blocks = v.reshape(v.shape[:-1] + (-1, 32))
    amax = np.abs(blocks).max(-1, keepdims=True)
    byte = np.maximum(np.where(amax > 0, np.frexp(amax)[1] - 1 + 127, 0) - down, 1)
    scale = np.exp2(byte - 127.0)
    codes = (blocks / scale).astype(np.float32).astype(dtype).astype(np.float64)
    return np.moveaxis((codes * scale).reshape(v.shape), -1, axis)


WIDE = False


def mx_kscale(k):
    if not WIDE:
        return np.ones(k)
    levels = np.array([10, -10, 5, -5, 0])
    if k % 512:
        return np.exp2(np.random.permutation(np.resize(levels, k // 32))).repeat(32)
    a = np.empty((k // 512, 16))
    for p in range(k // 512):
        a[p, :8] = np.random.permutation(np.resize(levels, 8))
        for g in range(8):
            far = levels[np.abs(levels - a[p, g]) >= 10]
            a[p, g + 8] = far[np.random.randint(len(far))]
    return np.exp2(a.ravel()).repeat(32)


def f64(x):
    return np.asarray(x).astype(np.float64)


def striped(idx):
    return np.tile(idx.reshape(-1, 16).T, (8, 1)).astype(np.uint16)


def unstriped(offs):
    return offs[:16].T.reshape(-1).astype(np.int64)


def striped8(idx):
    return np.concatenate([x.reshape(-1, 16).T for x in idx]).astype(np.uint16)


def runs(offs, k):
    lists = np.stack([offs[16 * r : 16 * r + 16].T.reshape(-1) for r in range(8)]).astype(np.int64)
    return lists[np.arange(k) % 512 // 64]


def pack_weight(w):
    k, n = w.shape
    w = f64(np.asarray(w, np.float32).astype(ml_dtypes.bfloat16)).reshape(k // 32, 32, n)
    amax = np.abs(w).max(1)
    byte = np.clip(np.where(amax > 0, np.frexp(amax)[1] - 1 + 127 - 7, 1), 1, 254)
    scaled = (w * np.exp2(127.0 - byte)[:, None, :]).reshape(k, n).astype(np.float32)
    words = np.ascontiguousarray(scaled.reshape(k // 512, 128, 4, n).transpose(0, 1, 3, 2)).astype(ml_dtypes.float8_e4m3fn).view(np.uint8)
    return words, np.ascontiguousarray(byte.astype(np.uint8).reshape(k // 512, 16, n))


def unpack_weight(words, scales):
    g, p, n, _ = words.shape
    vals = np.ascontiguousarray(words).view(ml_dtypes.float8_e4m3fn).astype(np.float64) * np.repeat(np.exp2(scales.astype(np.float64) - 127.0), 8, axis=1)[..., None]
    return vals.transpose(0, 1, 3, 2).reshape(g * 512, n)


def sigmoid(v):
    return 1.0 / (1.0 + np.exp(-np.maximum(v, -700.0)))


K, T, S, H, C, W = 512, 2048, 512, 512, 512, 256


def setup_inputs():
    n = np.random.standard_normal
    s = mx_kscale(K)[:, None]
    packed_xT = pack_weight(n((K, T)) * s)
    perm = np.stack([np.random.permutation(S) for _ in range(8)])
    return {
        "x_words": packed_xT[0],
        "x_scales": packed_xT[1],
        "w1": (n((K, H)) / np.sqrt(K) / s).astype(np.float32),
        "w2": (n((K, H)) / np.sqrt(K) / s).astype(np.float32),
        "gs": (np.random.uniform(0.5, 1.5, (K, 1)) / s).astype(np.float32),
        "offs": striped(np.random.permutation(T)[:S]),
        "two": striped(np.random.permutation(T)[:S]),
        "n1": striped8(np.stack([np.random.permutation(S) for _ in range(8)])),
        "n2": striped8(np.stack([np.random.permutation(S) for _ in range(8)])),
        "n3": striped8(np.stack([np.random.permutation(S) for _ in range(8)])),
        "cand": striped(np.random.permutation(T)[:C]),
        "n4": striped8(perm[:, :W]),
        "n5": striped8(perm[:, W:]),
    }


def reference(x_words, x_scales, w1, w2, gs, offs, two, n1, n2, n3, cand, n4, n5):
    x_cand = unpack_weight(x_words, x_scales)[:, unstriped(cand)]
    xq = unpack_weight(x_words, x_scales)[:, unstriped(offs)]
    y = mxq(f64(w1), 0, "e4m3").T @ xq
    x_two = unpack_weight(x_words, x_scales)[:, unstriped(two)]
    d = mxq(f64(w2), 0, "e4m3").T @ x_two
    z = f64(gs) * (np.maximum(np.minimum(y - (0.5 * (y[np.arange(H)[:, None], runs(n1, H)])), d[np.arange(H)[:, None], runs(n2, H)]), d[np.arange(H)[:, None], runs(n3, H)]))
    s = 0.0625 * ((x_cand.T @ mxq(z, 0, "e4m3")))
    pb = s[np.arange(C)[:, None], runs(n5, C)]
    pa = s[np.arange(C)[:, None], runs(n4, C)]
    rb = pb * sigmoid(pb - pa)
    ra = pa * sigmoid(pa - pb)
    ds = np.zeros((C, S))
    ds[np.arange(C)[:, None], runs(n4, C)] = ra
    out = ds.copy()
    out[np.arange(C)[:, None], runs(n5, C)] = rb
    return out

@@ -1,0 +1,169 @@
+from contextlib import ExitStack
+
+import concourse.mybir as mybir
+
+K, T, S, H, C, W = 512, 2048, 512, 512, 512, 256
+FLOPS = 2 * K * H * S * 2 + 2 * K * C * S
+
+F32 = mybir.dt.float32
+BF16 = mybir.dt.bfloat16
+I32 = mybir.dt.int32
+U32 = mybir.dt.uint32
+U16 = mybir.dt.uint16
+U8 = mybir.dt.uint8
+FP8X4 = mybir.dt.float8_e4m3fn_x4
+ALU = mybir.AluOpType
+ACT = mybir.ActivationFunctionType
+
+P = 128
+PACK = 4
+HALF = S // 2
+LCOLS = HALF // 16
+
+
+def tile_picked_twcclampbduel_none_p_kernel(tc, x_words, x_scales, w1, w2, gs, offs, two, n1, n2, n3, cand, n4, n5, out):
+    nc = tc.nc
+    with ExitStack() as ctx:
+        keep = ctx.enter_context(tc.tile_pool(name="keep", bufs=1))
+        ring = ctx.enter_context(tc.tile_pool(name="ring", bufs=2))
+        psum = ctx.enter_context(tc.psum_pool(name="psum", bufs=4))
+
+        def load_list(src, name):
+            t = keep.tile(list(src.shape), U16, name=name)
+            nc.sync.dma_start(t[:], src)
+            return t
+
+        def load_weight(w, name):
+            halves = []
+            for h in range(2):
+                raw = keep.tile([P, PACK, HALF], F32, name=name + "_raw%d" % h)
+                nc.sync.dma_start(raw[:], w[:, h * HALF : (h + 1) * HALF].rearrange("(p j) c -> p j c", j=PACK))
+                halves.append(raw)
+            return halves
+
+        xs = keep.tile([P, T], U8, name="xs", align_bytes=64)
+        nc.vector.memset(xs[:].bitcast(I32), 0)
+        for q in range(4):
+            nc.scalar.dma_start(xs[32 * q : 32 * q + 4, :].bitcast(I32), x_scales[0, 4 * q : 4 * q + 4, :].bitcast(I32))
+        l_offs = load_list(offs, "l_offs")
+        l_two = load_list(two, "l_two")
+        l_cand = load_list(cand, "l_cand")
+        w1_raw = load_weight(w1, "w1")
+        xw = keep.tile([P, T], U32, name="xw", align_bytes=64)
+        nc.sync.dma_start(xw[:].bitcast(I32), x_words[0].rearrange("p n t -> p (n t)").bitcast(I32))
+        l_n1 = load_list(n1, "l_n1")
+        w2_raw = load_weight(w2, "w2")
+        l_n2 = load_list(n2, "l_n2")
+        l_n3 = load_list(n3, "l_n3")
+        gs_sb = keep.tile([P, PACK], F32, name="gs_sb")
+        nc.sync.dma_start(gs_sb[:], gs.rearrange("(p t) o -> p (t o)", t=PACK))
+        l_n4 = load_list(n4, "l_n4")
+        l_n5 = load_list(n5, "l_n5")
+
+        def gather_bytes(lst, name):
+            g = keep.tile([P, S], U8, name=name, align_bytes=64)
+            nc.vector.tensor_copy(g[:], xs[:].indirect(lst[:]))
+            return g
+
+        def gather_words(lst, name, tag):
+            g = keep.tile([P, S], U32, name=name, tag=tag, align_bytes=64)
+            nc.vector.tensor_copy(g[:], xw[:].indirect(lst[:]))
+            return g
+
+        def quantize_weight(halves, name):
+            wb = keep.tile([P, PACK * H], BF16, name=name + "_bf", align_bytes=64)
+            view = wb[:].rearrange("p (t m j) -> p m j t", t=PACK, j=PACK)
+            for h in range(2):
+                nc.scalar.copy(view[:, h * 64 : (h + 1) * 64], halves[h][:].rearrange("p j (m t) -> p m j t", t=PACK))
+            codes = keep.tile([P, H], U32, name=name + "_codes", align_bytes=64)
+            scales = keep.tile([P, H], U8, name=name + "_scales", align_bytes=64)
+            nc.vector.quantize_mx(out=codes[:].bitcast(FP8X4), scales=scales[:], in_=wb[:])
+            return codes, scales
+
+        def product(acc, lw, ls, t, rw, rs):
+            cols = slice(t * P, (t + 1) * P)
+            nc.tensor.matmul_mx(out=acc, lhsT=lw[:, cols].bitcast(FP8X4), lhsT_scale=ls[:, cols],
+                                rhs=rw.bitcast(FP8X4), rhs_scale=rs, start=True, stop=True)
+
+        def project(wq, xw_g, xs_g, name):
+            rows = []
+            for t in range(PACK):
+                acc = psum.tile([P, S], F32, name="acc")
+                product(acc[:], wq[0], wq[1], t, xw_g[:], xs_g[:])
+                r = keep.tile([P, S], F32, name=name + "%d" % t)
+                nc.scalar.copy(r[:], acc[:])
+                rows.append(r)
+            return rows
+
+        def fetch(dst, window, lst):
+            for h in range(2):
+                nc.vector.tensor_copy(dst[:, h * HALF : (h + 1) * HALF], window[:].indirect(lst[:, h * LCOLS : (h + 1) * LCOLS]))
+
+        offs_s = gather_bytes(l_offs, "offs_s")
+        two_s = gather_bytes(l_two, "two_s")
+        cand_s = gather_bytes(l_cand, "cand_s")
+        cand_sd = keep.tile([P, C], U8, name="cand_sd", align_bytes=64)
+        nc.vector.tensor_copy(cand_sd[:].rearrange("p (t m) -> p t m", t=PACK), cand_s[:].rearrange("p (m t) -> p t m", t=PACK))
+        w1q = quantize_weight(w1_raw, "w1")
+        offs_w = gather_words(l_offs, "offs_w", "offs_w")
+        y = project(w1q, offs_w, offs_s, "y")
+        two_w = gather_words(l_two, "two_w", "two_w")
+
+        a = []
+        for t in range(PACK):
+            g1 = ring.tile([P, S], F32, name="g1")
+            fetch(g1, y[t], l_n1)
+            at = keep.tile([P, S], F32, name="a%d" % t)
+            nc.vector.scalar_tensor_tensor(at[:], g1[:], -0.5, y[t][:], ALU.mult, ALU.add)
+            a.append(at)
+            if t == 1:
+                w2q = quantize_weight(w2_raw, "w2")
+                d = project(w2q, two_w, two_s, "d")
+
+        zb = keep.tile([P, S, PACK], BF16, name="zb", align_bytes=64)
+        for t in range(PACK):
+            g2 = ring.tile([P, S], F32, name="g2")
+            fetch(g2, d[t], l_n2)
+            if t == PACK - 1:
+                g3 = keep.tile([P, S], F32, name="g3_last", tag="late", align_bytes=64)
+            else:
+                g3 = ring.tile([P, S], F32, name="g3")
+            fetch(g3, d[t], l_n3)
+            m = ring.tile([P, S], F32, name="m")
+            nc.vector.tensor_tensor(m[:], a[t][:], g2[:], ALU.min)
+            zt = ring.tile([P, S], F32, name="zt")
+            nc.vector.tensor_tensor(zt[:], m[:], g3[:], ALU.max)
+            for h in range(2):
+                cols = slice(h * HALF, (h + 1) * HALF)
+                nc.scalar.activation(zb[:, cols, t], zt[:, cols], ACT.Copy, scale=gs_sb[:, t : t + 1])
+
+        cand_w = gather_words(l_cand, "cand_w", "late")
+        cand_wd = keep.tile([P, C], U32, name="cand_wd", align_bytes=64)
+        nc.vector.tensor_copy(cand_wd[:].rearrange("p (t m) -> p t m", t=PACK), cand_w[:].rearrange("p (m t) -> p t m", t=PACK))
+        z_w = keep.tile([P, S], U32, name="z_w", align_bytes=64)
+        z_s = keep.tile([P, S], U8, name="z_s", align_bytes=64)
+        for h in range(2):
+            cols = slice(h * HALF, (h + 1) * HALF)
+            nc.vector.quantize_mx(out=z_w[:, cols].bitcast(FP8X4), scales=z_s[:, cols],
+                                  in_=zb[:, cols, :].rearrange("p c t -> p (c t)"))
+
+        out_t = out.rearrange("(p t) c -> t p c", t=PACK)
+        for t in range(PACK):
+            acc = psum.tile([P, S], F32, name="acc")
+            product(acc[:], cand_wd, cand_sd, t, z_w[:], z_s[:])
+            s = keep.tile([P, S], F32, name="s%d" % t)
+            nc.scalar.activation(s[:], acc[:], ACT.Copy, scale=0.0625)
+            pa = keep.tile([P, W], F32, name="pa%d" % t)
+            pb = keep.tile([P, W], F32, name="pb%d" % t)
+            nc.vector.tensor_copy(pa[:], s[:].indirect(l_n4[:]))
+            nc.vector.tensor_copy(pb[:], s[:].indirect(l_n5[:]))
+            df = keep.tile([P, W], F32, name="df%d" % t)
+            nc.vector.tensor_tensor(df[:], pb[:], pa[:], ALU.subtract)
+            sa = keep.tile([P, W], F32, name="sa%d" % t)
+            sb = keep.tile([P, W], F32, name="sb%d" % t)
+            nc.scalar.activation(sa[:], df[:], ACT.Sigmoid, scale=-1.0)
+            nc.scalar.activation(sb[:], df[:], ACT.Sigmoid)
+            res = keep.tile([P, S], F32, name="res%d" % t)
+            nc.vector.tensor_tensor(res[:].indirect(l_n4[:]), pa[:], sa[:], ALU.mult)
+            nc.vector.tensor_tensor(res[:].indirect(l_n5[:]), pb[:], sb[:], ALU.mult)
+            nc.sync.dma_start(out_t[t], res[:])

@@ -1,6 +1,7 @@
 from contextlib import ExitStack
 
 import concourse.mybir as mybir
+from concourse.masks import make_identity
 
 K, T, S, H, C, W = 512, 2048, 512, 512, 512, 256
 FLOPS = 2 * K * H * S * 2 + 2 * K * C * S
@@ -18,7 +19,7 @@ ACT = mybir.ActivationFunctionType
 P = 128
 PACK = 4
 HALF = S // 2
-LCOLS = HALF // 16
+PIECES = [slice(0, 256), slice(256, 384), slice(384, 512)]
 
 
 def tile_picked_twcclampbduel_none_p_kernel(tc, x_words, x_scales, w1, w2, gs, offs, two, n1, n2, n3, cand, n4, n5, out):
@@ -26,7 +27,7 @@ def tile_picked_twcclampbduel_none_p_kernel(tc, x_words, x_scales, w1, w2, gs, o
     with ExitStack() as ctx:
         keep = ctx.enter_context(tc.tile_pool(name="keep", bufs=1))
         ring = ctx.enter_context(tc.tile_pool(name="ring", bufs=2))
-        psum = ctx.enter_context(tc.psum_pool(name="psum", bufs=4))
+        psum = ctx.enter_context(tc.psum_pool(name="psum", bufs=2))
 
         def load_list(src, name):
             t = keep.tile(list(src.shape), U16, name=name)
@@ -36,29 +37,37 @@ def tile_picked_twcclampbduel_none_p_kernel(tc, x_words, x_scales, w1, w2, gs, o
         def load_weight(w, name):
             halves = []
             for h in range(2):
-                raw = keep.tile([P, PACK, HALF], F32, name=name + "_raw%d" % h)
+                raw = keep.tile([P, PACK, HALF], F32, name=name + "_raw%d" % h, tag=name + "_raw%d" % h)
                 nc.sync.dma_start(raw[:], w[:, h * HALF : (h + 1) * HALF].rearrange("(p j) c -> p j c", j=PACK))
                 halves.append(raw)
             return halves
 
         xs = keep.tile([P, T], U8, name="xs", align_bytes=64)
-        nc.vector.memset(xs[:].bitcast(I32), 0)
+        nc.gpsimd.memset(xs[:].bitcast(I32), 0)
         for q in range(4):
-            nc.scalar.dma_start(xs[32 * q : 32 * q + 4, :].bitcast(I32), x_scales[0, 4 * q : 4 * q + 4, :].bitcast(I32))
+            nc.sync.dma_start(xs[32 * q : 32 * q + 4, :].bitcast(I32), x_scales[0, 4 * q : 4 * q + 4, :].bitcast(I32))
         l_offs = load_list(offs, "l_offs")
         l_two = load_list(two, "l_two")
         l_cand = load_list(cand, "l_cand")
         w1_raw = load_weight(w1, "w1")
         xw = keep.tile([P, T], U32, name="xw", align_bytes=64)
         nc.sync.dma_start(xw[:].bitcast(I32), x_words[0].rearrange("p n t -> p (n t)").bitcast(I32))
-        l_n1 = load_list(n1, "l_n1")
         w2_raw = load_weight(w2, "w2")
+        l_n1 = load_list(n1, "l_n1")
         l_n2 = load_list(n2, "l_n2")
         l_n3 = load_list(n3, "l_n3")
         gs_sb = keep.tile([P, PACK], F32, name="gs_sb")
         nc.sync.dma_start(gs_sb[:], gs.rearrange("(p t) o -> p (t o)", t=PACK))
         l_n4 = load_list(n4, "l_n4")
         l_n5 = load_list(n5, "l_n5")
+        ident = keep.tile([P, P], F32, name="ident")
+        make_identity(nc, ident[:])
+
+        y = []
+        for t in range(PACK):
+            yt = keep.tile([P, 2 * S], F32, name="y%d" % t, tag="y%d" % t, align_bytes=64)
+            nc.gpsimd.memset(yt[:, S:], 0.0)
+            y.append(yt)
 
         def gather_bytes(lst, name):
             g = keep.tile([P, S], U8, name=name, align_bytes=64)
@@ -70,11 +79,14 @@ def tile_picked_twcclampbduel_none_p_kernel(tc, x_words, x_scales, w1, w2, gs, o
             nc.vector.tensor_copy(g[:], xw[:].indirect(lst[:]))
             return g
 
-        def quantize_weight(halves, name):
-            wb = keep.tile([P, PACK * H], BF16, name=name + "_bf", align_bytes=64)
+        def cast_weight(halves, name):
+            wb = keep.tile([P, PACK * H], BF16, name=name + "_bf", tag=name + "_bf", align_bytes=64)
             view = wb[:].rearrange("p (t m j) -> p m j t", t=PACK, j=PACK)
             for h in range(2):
                 nc.scalar.copy(view[:, h * 64 : (h + 1) * 64], halves[h][:].rearrange("p j (m t) -> p m j t", t=PACK))
+            return wb
+
+        def quantize_weight(wb, name):
             codes = keep.tile([P, H], U32, name=name + "_codes", align_bytes=64)
             scales = keep.tile([P, H], U8, name=name + "_scales", align_bytes=64)
             nc.vector.quantize_mx(out=codes[:].bitcast(FP8X4), scales=scales[:], in_=wb[:])
@@ -82,88 +94,110 @@ def tile_picked_twcclampbduel_none_p_kernel(tc, x_words, x_scales, w1, w2, gs, o
 
         def product(acc, lw, ls, t, rw, rs):
             cols = slice(t * P, (t + 1) * P)
-            nc.tensor.matmul_mx(out=acc, lhsT=lw[:, cols].bitcast(FP8X4), lhsT_scale=ls[:, cols],
+            nc.tensor.matmul_mx(out=acc, lhsT=lw.bitcast(FP8X4), lhsT_scale=ls[:, cols],
                                 rhs=rw.bitcast(FP8X4), rhs_scale=rs, start=True, stop=True)
 
-        def project(wq, xw_g, xs_g, name):
-            rows = []
-            for t in range(PACK):
-                acc = psum.tile([P, S], F32, name="acc")
-                product(acc[:], wq[0], wq[1], t, xw_g[:], xs_g[:])
-                r = keep.tile([P, S], F32, name=name + "%d" % t)
-                nc.scalar.copy(r[:], acc[:])
-                rows.append(r)
-            return rows
+        def project(wq, xw_g, xs_g, t, dst):
+            acc = psum.tile([P, S], F32, name="acc", tag="acc", bufs=3)
+            product(acc[:], wq[0][:, t * P : (t + 1) * P], wq[1], t, xw_g[:], xs_g[:])
+            nc.scalar.copy(dst, acc[:])
 
-        def fetch(dst, window, lst):
-            for h in range(2):
-                nc.vector.tensor_copy(dst[:, h * HALF : (h + 1) * HALF], window[:].indirect(lst[:, h * LCOLS : (h + 1) * LCOLS]))
+        def turn_sum(terms, width, tag, bufs):
+            acc = psum.tile([P, width], F32, name=tag, tag=tag, bufs=bufs)
+            for b in range(width // P):
+                cols = slice(b * P, (b + 1) * P)
+                for i, u in enumerate(terms):
+                    nc.tensor.matmul(acc[:, cols], u[:, cols], ident[:], start=(i == 0), stop=(i == len(terms) - 1), is_transpose=True)
+            return acc
 
         offs_s = gather_bytes(l_offs, "offs_s")
         two_s = gather_bytes(l_two, "two_s")
         cand_s = gather_bytes(l_cand, "cand_s")
-        cand_sd = keep.tile([P, C], U8, name="cand_sd", align_bytes=64)
-        nc.vector.tensor_copy(cand_sd[:].rearrange("p (t m) -> p t m", t=PACK), cand_s[:].rearrange("p (m t) -> p t m", t=PACK))
-        w1q = quantize_weight(w1_raw, "w1")
+        w1q = quantize_weight(cast_weight(w1_raw, "w1"), "w1")
         offs_w = gather_words(l_offs, "offs_w", "offs_w")
-        y = project(w1q, offs_w, offs_s, "y")
         two_w = gather_words(l_two, "two_w", "two_w")
+        cand_sd = keep.tile([P, C], U8, name="cand_sd", tag="w1_bf", align_bytes=64)
+        nc.vector.tensor_copy(cand_sd[:].rearrange("p (t m) -> p t m", t=PACK), cand_s[:].rearrange("p (m t) -> p t m", t=PACK))
 
-        a = []
+        d, a = [], []
         for t in range(PACK):
-            g1 = ring.tile([P, S], F32, name="g1")
-            fetch(g1, y[t], l_n1)
-            at = keep.tile([P, S], F32, name="a%d" % t)
-            nc.vector.scalar_tensor_tensor(at[:], g1[:], -0.5, y[t][:], ALU.mult, ALU.add)
-            a.append(at)
-            if t == 1:
-                w2q = quantize_weight(w2_raw, "w2")
-                d = project(w2q, two_w, two_s, "d")
+            if t == 2:
+                w2q = quantize_weight(cast_weight(w2_raw, "w2"), "w2")
+            project(w1q, offs_w, offs_s, t, y[t][:, :S])
+            dt = keep.tile([P, 2 * S], F32, name="d%d" % t, tag="w2_bf" if t == 2 else "d%d" % t, align_bytes=64)
+            nc.vector.tensor_scalar(dt[:, S:], y[t][:].indirect(l_n1[:]), -0.5, 0.0, ALU.mult, ALU.add)
+            d.append(dt)
 
-        zb = keep.tile([P, S, PACK], BF16, name="zb", align_bytes=64)
+        def less_half(t):
+            turned = keep.tile([P, S], F32, name="turned%d" % t)
+            nc.scalar.copy(turned[:], turn_sum([y[t][:, :S], d[t][:, S:]], S, "duel", 2)[:])
+            a.append(turn_sum([turned[:]], S, "gap", 3))
+
         for t in range(PACK):
-            g2 = ring.tile([P, S], F32, name="g2")
-            fetch(g2, d[t], l_n2)
-            if t == PACK - 1:
-                g3 = keep.tile([P, S], F32, name="g3_last", tag="late", align_bytes=64)
-            else:
-                g3 = ring.tile([P, S], F32, name="g3")
-            fetch(g3, d[t], l_n3)
-            m = ring.tile([P, S], F32, name="m")
-            nc.vector.tensor_tensor(m[:], a[t][:], g2[:], ALU.min)
-            zt = ring.tile([P, S], F32, name="zt")
+            less_half(t)
+        for t in range(PACK):
+            project(w2q, two_w, two_s, t, d[t][:, :S])
+
+        zb = keep.tile([P, S, PACK], BF16, name="zb", tag="zb", align_bytes=64)
+        for u in range(PACK):
+            g2 = keep.tile([P, S], F32, name="g2_%d" % u, tag="g2_%d" % u, align_bytes=64)
+            nc.vector.tensor_copy(g2[:], d[u][:].indirect(l_n2[:]))
+            g3 = keep.tile([P, S], F32, name="g3_%d" % u, tag="g3_%d" % u, align_bytes=64)
+            nc.vector.tensor_copy(g3[:], d[u][:].indirect(l_n3[:]))
+            m = keep.tile([P, S], F32, name="m%d" % u)
+            nc.vector.tensor_tensor(m[:], g2[:], a[u][:], ALU.min)
+            zt = keep.tile([P, S], F32, name="zt%d" % u)
             nc.vector.tensor_tensor(zt[:], m[:], g3[:], ALU.max)
-            for h in range(2):
-                cols = slice(h * HALF, (h + 1) * HALF)
-                nc.scalar.activation(zb[:, cols, t], zt[:, cols], ACT.Copy, scale=gs_sb[:, t : t + 1])
+            for cols in PIECES if u == PACK - 1 else [slice(0, S)]:
+                nc.scalar.activation(zb[:, cols, u], zt[:, cols], ACT.Copy, scale=gs_sb[:, u : u + 1])
+        cand_w = gather_words(l_cand, "cand_w", "g2_3")
 
-        cand_w = gather_words(l_cand, "cand_w", "late")
-        cand_wd = keep.tile([P, C], U32, name="cand_wd", align_bytes=64)
-        nc.vector.tensor_copy(cand_wd[:].rearrange("p (t m) -> p t m", t=PACK), cand_w[:].rearrange("p (m t) -> p t m", t=PACK))
+        cand_rows = cand_w[:].rearrange("p (m t) -> p t m", t=PACK)
+        cand_first = keep.tile([P, P], U32, name="cand_first", align_bytes=64)
+        nc.vector.tensor_copy(cand_first[:], cand_rows[:, 0, :])
         z_w = keep.tile([P, S], U32, name="z_w", align_bytes=64)
         z_s = keep.tile([P, S], U8, name="z_s", align_bytes=64)
-        for h in range(2):
-            cols = slice(h * HALF, (h + 1) * HALF)
+        for cols in PIECES:
             nc.vector.quantize_mx(out=z_w[:, cols].bitcast(FP8X4), scales=z_s[:, cols],
                                   in_=zb[:, cols, :].rearrange("p c t -> p (c t)"))
 
+        cand_rest = keep.tile([P, PACK - 1, P], U32, name="cand_rest", tag="zb", align_bytes=64)
+        nc.vector.tensor_copy(cand_rest[:], cand_rows[:, 1:, :])
+        cand_wd = [cand_first[:]] + [cand_rest[:, t, :] for t in range(PACK - 1)]
+
         out_t = out.rearrange("(p t) c -> t p c", t=PACK)
+        scores = []
         for t in range(PACK):
-            acc = psum.tile([P, S], F32, name="acc")
-            product(acc[:], cand_wd, cand_sd, t, z_w[:], z_s[:])
-            s = keep.tile([P, S], F32, name="s%d" % t)
-            nc.scalar.activation(s[:], acc[:], ACT.Copy, scale=0.0625)
-            pa = keep.tile([P, W], F32, name="pa%d" % t)
+            s = keep.tile([P, S], F32, name="s%d" % t, tag="s%d" % t)
+            for cols in PIECES if t == 0 else [slice(0, S)]:
+                acc = psum.tile([P, cols.stop - cols.start], F32, name="acc", tag="acc", bufs=3)
+                product(acc[:], cand_wd[t], cand_sd, t, z_w[:, cols], z_s[:, cols])
+                nc.scalar.activation(s[:, cols], acc[:], ACT.Copy, scale=0.0625)
+            scores.append(s)
+        duel = []
+        for t in range(PACK):
+            s = scores[t]
+            pan = keep.tile([P, W], F32, name="pan%d" % t)
             pb = keep.tile([P, W], F32, name="pb%d" % t)
-            nc.vector.tensor_copy(pa[:], s[:].indirect(l_n4[:]))
+            nc.vector.tensor_scalar(pan[:], s[:].indirect(l_n4[:]), -1.0, 0.0, ALU.mult, ALU.add)
             nc.vector.tensor_copy(pb[:], s[:].indirect(l_n5[:]))
-            df = keep.tile([P, W], F32, name="df%d" % t)
-            nc.vector.tensor_tensor(df[:], pb[:], pa[:], ALU.subtract)
-            sa = keep.tile([P, W], F32, name="sa%d" % t)
+            staged = keep.tile([P, W], F32, name="staged%d" % t, tag="staged%d" % t)
+            nc.scalar.copy(staged[:], turn_sum([pb[:], pan[:]], W, "duel", 2)[:])
+            df = turn_sum([staged[:]], W, "gap", 3)
+            th = keep.tile([P, W], F32, name="th%d" % t, tag="th%d" % t)
+            nc.scalar.activation(th[:], df[:], ACT.Tanh, scale=0.5)
             sb = keep.tile([P, W], F32, name="sb%d" % t)
-            nc.scalar.activation(sa[:], df[:], ACT.Sigmoid, scale=-1.0)
-            nc.scalar.activation(sb[:], df[:], ACT.Sigmoid)
-            res = keep.tile([P, S], F32, name="res%d" % t)
-            nc.vector.tensor_tensor(res[:].indirect(l_n4[:]), pa[:], sa[:], ALU.mult)
-            nc.vector.tensor_tensor(res[:].indirect(l_n5[:]), pb[:], sb[:], ALU.mult)
-            nc.sync.dma_start(out_t[t], res[:])
+            nc.scalar.activation(sb[:], th[:], ACT.Copy, scale=0.5, bias=0.5)
+            duel.append((pan, th, pb, sb))
+        for pair in ((0, 1), (2, 3)):
+            res = {}
+            for t in pair:
+                pan, th, pb, sb = duel[t]
+                res[t] = keep.tile([P, S], F32, name="res%d" % t, tag="s%d" % (PACK - 1 - t))
+                nc.vector.tensor_tensor(res[t][:].indirect(l_n5[:]), pb[:], sb[:], ALU.mult)
+            for t in pair:
+                pan, th, pb, sb = duel[t]
+                san = keep.tile([P, W], F32, name="san%d" % t, tag="th%d" % (pair[1] + pair[0] - t))
+                nc.scalar.activation(san[:], sb[:], ACT.Copy, bias=-1.0)
+                nc.vector.tensor_tensor(res[t][:].indirect(l_n4[:]), pan[:], san[:], ALU.mult)
+                nc.sync.dma_start(out_t[t], res[t][:])

@@ -63,11 +63,10 @@ def tile_picked_twcclampbduel_none_p_kernel(tc, x_words, x_scales, w1, w2, gs, o
         ident = keep.tile([P, P], F32, name="ident")
         make_identity(nc, ident[:])
 
-        y = []
-        for t in range(PACK):
-            yt = keep.tile([P, 2 * S], F32, name="y%d" % t, tag="y%d" % t, align_bytes=64)
-            nc.gpsimd.memset(yt[:, S:], 0.0)
-            y.append(yt)
+        half_y = [keep.tile([P, 2 * S], F32, name="half_y%d" % t) for t in range(PACK)]
+        nc.gpsimd.memset(half_y[0][:, S:], 0.0)
+        y_last = keep.tile([P, S], F32, name="y_last")
+        y = [half_y[t + 1][:, S:] for t in range(PACK - 1)] + [y_last[:]]
 
         def gather_bytes(lst, name):
             g = keep.tile([P, S], U8, name=name, align_bytes=64)
@@ -119,24 +118,33 @@ def tile_picked_twcclampbduel_none_p_kernel(tc, x_words, x_scales, w1, w2, gs, o
         cand_sd = keep.tile([P, C], U8, name="cand_sd", tag="w1_bf", align_bytes=64)
         nc.vector.tensor_copy(cand_sd[:].rearrange("p (t m) -> p t m", t=PACK), cand_s[:].rearrange("p (m t) -> p t m", t=PACK))
 
-        d, a = [], []
-        for t in range(PACK):
-            if t == 2:
-                w2q = quantize_weight(cast_weight(w2_raw, "w2"), "w2")
-            project(w1q, offs_w, offs_s, t, y[t][:, :S])
+        d, a, y_acc = [], [], []
+
+        def first_product(t):
+            acc = psum.tile([P, S], F32, name="acc", tag="acc", bufs=3)
+            product(acc[:], w1q[0][:, t * P : (t + 1) * P], w1q[1], t, offs_w[:], offs_s[:])
+            nc.scalar.activation(half_y[t][:, :S], acc[:], ACT.Copy, scale=-0.5)
+            y_acc.append(acc)
             dt = keep.tile([P, 2 * S], F32, name="d%d" % t, tag="w2_bf" if t == 2 else "d%d" % t, align_bytes=64)
-            nc.vector.tensor_scalar(dt[:, S:], y[t][:].indirect(l_n1[:]), -0.5, 0.0, ALU.mult, ALU.add)
+            nc.vector.tensor_copy(dt[:, S:], half_y[t][:].indirect(l_n1[:]))
             d.append(dt)
 
         def less_half(t):
             turned = keep.tile([P, S], F32, name="turned%d" % t)
-            nc.scalar.copy(turned[:], turn_sum([y[t][:, :S], d[t][:, S:]], S, "duel", 2)[:])
+            nc.scalar.copy(turned[:], turn_sum([y[t], d[t][:, S:]], S, "duel", 2)[:])
             a.append(turn_sum([turned[:]], S, "gap", 3))
 
         for t in range(PACK):
-            less_half(t)
+            if t == 2:
+                w2q = quantize_weight(cast_weight(w2_raw, "w2"), "w2")
+            if t > 0:
+                nc.scalar.copy(y[t - 1], y_acc[t - 1][:])
+            first_product(t)
         for t in range(PACK):
             project(w2q, two_w, two_s, t, d[t][:, :S])
+            if t == 0:
+                nc.scalar.copy(y[PACK - 1], y_acc[PACK - 1][:])
+            less_half(t)
 
         zb = keep.tile([P, S, PACK], BF16, name="zb", tag="zb", align_bytes=64)
         for u in range(PACK):
@@ -182,10 +190,8 @@ def tile_picked_twcclampbduel_none_p_kernel(tc, x_words, x_scales, w1, w2, gs, o
             nc.vector.tensor_scalar(pan[:], s[:].indirect(l_n4[:]), -1.0, 0.0, ALU.mult, ALU.add)
             nc.vector.tensor_copy(pb[:], s[:].indirect(l_n5[:]))
             staged = keep.tile([P, W], F32, name="staged%d" % t, tag="staged%d" % t)
-            nc.scalar.copy(staged[:], turn_sum([pb[:], pan[:]], W, "duel", 2)[:])
-            df = turn_sum([staged[:]], W, "gap", 3)
-            th = keep.tile([P, W], F32, name="th%d" % t, tag="th%d" % t)
-            nc.scalar.activation(th[:], df[:], ACT.Tanh, scale=0.5)
+            nc.scalar.activation(staged[:], turn_sum([pb[:], pan[:]], W, "duel", 2)[:], ACT.Tanh, scale=0.5)
+            th = turn_sum([staged[:]], W, "gap", 3)
             sb = keep.tile([P, W], F32, name="sb%d" % t)
             nc.scalar.activation(sb[:], th[:], ACT.Copy, scale=0.5, bias=0.5)
             duel.append((pan, th, pb, sb))
@@ -197,7 +203,7 @@ def tile_picked_twcclampbduel_none_p_kernel(tc, x_words, x_scales, w1, w2, gs, o
                 nc.vector.tensor_tensor(res[t][:].indirect(l_n5[:]), pb[:], sb[:], ALU.mult)
             for t in pair:
                 pan, th, pb, sb = duel[t]
-                san = keep.tile([P, W], F32, name="san%d" % t, tag="th%d" % (pair[1] + pair[0] - t))
+                san = keep.tile([P, W], F32, name="san%d" % t, tag="staged%d" % (pair[1] + pair[0] - t))
                 nc.scalar.activation(san[:], sb[:], ACT.Copy, bias=-1.0)
                 nc.vector.tensor_tensor(res[t][:].indirect(l_n4[:]), pan[:], san[:], ALU.mult)
                 nc.sync.dma_start(out_t[t], res[t][:])

from contextlib import ExitStack

import concourse.mybir as mybir
from concourse.masks import make_identity

K, T, S, H, C, W = 512, 2048, 512, 512, 512, 256
FLOPS = 2 * K * H * S * 2 + 2 * K * C * S

F32 = mybir.dt.float32
BF16 = mybir.dt.bfloat16
I32 = mybir.dt.int32
U32 = mybir.dt.uint32
U16 = mybir.dt.uint16
U8 = mybir.dt.uint8
FP8X4 = mybir.dt.float8_e4m3fn_x4
ALU = mybir.AluOpType
ACT = mybir.ActivationFunctionType

P = 128
PACK = 4
HALF = S // 2
PIECES = [slice(0, 256), slice(256, 384), slice(384, 512)]


def tile_picked_twcclampbduel_none_p_kernel(tc, x_words, x_scales, w1, w2, gs, offs, two, n1, n2, n3, cand, n4, n5, out):
    nc = tc.nc
    with ExitStack() as ctx:
        keep = ctx.enter_context(tc.tile_pool(name="keep", bufs=1))
        ring = ctx.enter_context(tc.tile_pool(name="ring", bufs=2))
        psum = ctx.enter_context(tc.psum_pool(name="psum", bufs=2))

        def load_list(src, name):
            t = keep.tile(list(src.shape), U16, name=name)
            nc.sync.dma_start(t[:], src)
            return t

        def load_weight(w, name):
            halves = []
            for h in range(2):
                raw = keep.tile([P, PACK, HALF], F32, name=name + "_raw%d" % h, tag=name + "_raw%d" % h)
                nc.sync.dma_start(raw[:], w[:, h * HALF : (h + 1) * HALF].rearrange("(p j) c -> p j c", j=PACK))
                halves.append(raw)
            return halves

        xs = keep.tile([P, T], U8, name="xs", align_bytes=64)
        nc.gpsimd.memset(xs[:].bitcast(I32), 0)
        for q in range(4):
            nc.sync.dma_start(xs[32 * q : 32 * q + 4, :].bitcast(I32), x_scales[0, 4 * q : 4 * q + 4, :].bitcast(I32))
        l_offs = load_list(offs, "l_offs")
        l_two = load_list(two, "l_two")
        l_cand = load_list(cand, "l_cand")
        w1_raw = load_weight(w1, "w1")
        xw = keep.tile([P, T], U32, name="xw", align_bytes=64)
        nc.sync.dma_start(xw[:].bitcast(I32), x_words[0].rearrange("p n t -> p (n t)").bitcast(I32))
        w2_raw = load_weight(w2, "w2")
        l_n1 = load_list(n1, "l_n1")
        l_n2 = load_list(n2, "l_n2")
        l_n3 = load_list(n3, "l_n3")
        gs_sb = keep.tile([P, PACK], F32, name="gs_sb")
        nc.sync.dma_start(gs_sb[:], gs.rearrange("(p t) o -> p (t o)", t=PACK))
        l_n4 = load_list(n4, "l_n4")
        l_n5 = load_list(n5, "l_n5")
        ident = keep.tile([P, P], F32, name="ident")
        make_identity(nc, ident[:])

        half_y = [keep.tile([P, 2 * S], F32, name="half_y%d" % t) for t in range(PACK)]
        nc.gpsimd.memset(half_y[0][:, S:], 0.0)
        y_last = keep.tile([P, S], F32, name="y_last")
        y = [half_y[t + 1][:, S:] for t in range(PACK - 1)] + [y_last[:]]

        def gather_bytes(lst, name):
            g = keep.tile([P, S], U8, name=name, align_bytes=64)
            nc.vector.tensor_copy(g[:], xs[:].indirect(lst[:]))
            return g

        def gather_words(lst, name, tag):
            g = keep.tile([P, S], U32, name=name, tag=tag, align_bytes=64)
            nc.vector.tensor_copy(g[:], xw[:].indirect(lst[:]))
            return g

        def cast_weight(halves, name):
            wb = keep.tile([P, PACK * H], BF16, name=name + "_bf", tag=name + "_bf", align_bytes=64)
            view = wb[:].rearrange("p (t m j) -> p m j t", t=PACK, j=PACK)
            for h in range(2):
                nc.scalar.copy(view[:, h * 64 : (h + 1) * 64], halves[h][:].rearrange("p j (m t) -> p m j t", t=PACK))
            return wb

        def quantize_weight(wb, name):
            codes = keep.tile([P, H], U32, name=name + "_codes", align_bytes=64)
            scales = keep.tile([P, H], U8, name=name + "_scales", align_bytes=64)
            nc.vector.quantize_mx(out=codes[:].bitcast(FP8X4), scales=scales[:], in_=wb[:])
            return codes, scales

        def product(acc, lw, ls, t, rw, rs):
            cols = slice(t * P, (t + 1) * P)
            nc.tensor.matmul_mx(out=acc, lhsT=lw.bitcast(FP8X4), lhsT_scale=ls[:, cols],
                                rhs=rw.bitcast(FP8X4), rhs_scale=rs, start=True, stop=True)

        def project(wq, xw_g, xs_g, t, dst):
            acc = psum.tile([P, S], F32, name="acc", tag="acc", bufs=3)
            product(acc[:], wq[0][:, t * P : (t + 1) * P], wq[1], t, xw_g[:], xs_g[:])
            nc.scalar.copy(dst, acc[:])

        def turn_sum(terms, width, tag, bufs):
            acc = psum.tile([P, width], F32, name=tag, tag=tag, bufs=bufs)
            for b in range(width // P):
                cols = slice(b * P, (b + 1) * P)
                for i, u in enumerate(terms):
                    nc.tensor.matmul(acc[:, cols], u[:, cols], ident[:], start=(i == 0), stop=(i == len(terms) - 1), is_transpose=True)
            return acc

        offs_s = gather_bytes(l_offs, "offs_s")
        two_s = gather_bytes(l_two, "two_s")
        cand_s = gather_bytes(l_cand, "cand_s")
        w1q = quantize_weight(cast_weight(w1_raw, "w1"), "w1")
        offs_w = gather_words(l_offs, "offs_w", "offs_w")
        two_w = gather_words(l_two, "two_w", "two_w")
        cand_sd = keep.tile([P, C], U8, name="cand_sd", tag="w1_bf", align_bytes=64)
        nc.vector.tensor_copy(cand_sd[:].rearrange("p (t m) -> p t m", t=PACK), cand_s[:].rearrange("p (m t) -> p t m", t=PACK))

        d, a, y_acc = [], [], []

        def first_product(t):
            acc = psum.tile([P, S], F32, name="acc", tag="acc", bufs=3)
            product(acc[:], w1q[0][:, t * P : (t + 1) * P], w1q[1], t, offs_w[:], offs_s[:])
            nc.scalar.activation(half_y[t][:, :S], acc[:], ACT.Copy, scale=-0.5)
            y_acc.append(acc)
            dt = keep.tile([P, 2 * S], F32, name="d%d" % t, tag="w2_bf" if t == 2 else "d%d" % t, align_bytes=64)
            nc.vector.tensor_copy(dt[:, S:], half_y[t][:].indirect(l_n1[:]))
            d.append(dt)

        def less_half(t):
            turned = keep.tile([P, S], F32, name="turned%d" % t)
            nc.scalar.copy(turned[:], turn_sum([y[t], d[t][:, S:]], S, "duel", 2)[:])
            a.append(turn_sum([turned[:]], S, "gap", 3))

        for t in range(PACK):
            if t == 2:
                w2q = quantize_weight(cast_weight(w2_raw, "w2"), "w2")
            if t > 0:
                nc.scalar.copy(y[t - 1], y_acc[t - 1][:])
            first_product(t)
        for t in range(PACK):
            project(w2q, two_w, two_s, t, d[t][:, :S])
            if t == 0:
                nc.scalar.copy(y[PACK - 1], y_acc[PACK - 1][:])
            less_half(t)

        zb = keep.tile([P, S, PACK], BF16, name="zb", tag="zb", align_bytes=64)
        for u in range(PACK):
            g2 = keep.tile([P, S], F32, name="g2_%d" % u, tag="g2_%d" % u, align_bytes=64)
            nc.vector.tensor_copy(g2[:], d[u][:].indirect(l_n2[:]))
            g3 = keep.tile([P, S], F32, name="g3_%d" % u, tag="g3_%d" % u, align_bytes=64)
            nc.vector.tensor_copy(g3[:], d[u][:].indirect(l_n3[:]))
            m = keep.tile([P, S], F32, name="m%d" % u)
            nc.vector.tensor_tensor(m[:], g2[:], a[u][:], ALU.min)
            zt = keep.tile([P, S], F32, name="zt%d" % u)
            nc.vector.tensor_tensor(zt[:], m[:], g3[:], ALU.max)
            for cols in PIECES if u == PACK - 1 else [slice(0, S)]:
                nc.scalar.activation(zb[:, cols, u], zt[:, cols], ACT.Copy, scale=gs_sb[:, u : u + 1])
        cand_w = gather_words(l_cand, "cand_w", "g2_3")

        cand_rows = cand_w[:].rearrange("p (m t) -> p t m", t=PACK)
        cand_first = keep.tile([P, P], U32, name="cand_first", align_bytes=64)
        nc.vector.tensor_copy(cand_first[:], cand_rows[:, 0, :])
        z_w = keep.tile([P, S], U32, name="z_w", align_bytes=64)
        z_s = keep.tile([P, S], U8, name="z_s", align_bytes=64)
        for cols in PIECES:
            nc.vector.quantize_mx(out=z_w[:, cols].bitcast(FP8X4), scales=z_s[:, cols],
                                  in_=zb[:, cols, :].rearrange("p c t -> p (c t)"))

        cand_rest = keep.tile([P, PACK - 1, P], U32, name="cand_rest", tag="zb", align_bytes=64)
        nc.vector.tensor_copy(cand_rest[:], cand_rows[:, 1:, :])
        cand_wd = [cand_first[:]] + [cand_rest[:, t, :] for t in range(PACK - 1)]

        out_t = out.rearrange("(p t) c -> t p c", t=PACK)
        scores = []
        for t in range(PACK):
            s = keep.tile([P, S], F32, name="s%d" % t, tag="s%d" % t)
            for cols in PIECES if t == 0 else [slice(0, S)]:
                acc = psum.tile([P, cols.stop - cols.start], F32, name="acc", tag="acc", bufs=3)
                product(acc[:], cand_wd[t], cand_sd, t, z_w[:, cols], z_s[:, cols])
                nc.scalar.activation(s[:, cols], acc[:], ACT.Copy, scale=0.0625)
            scores.append(s)
        duel = []
        for t in range(PACK):
            s = scores[t]
            pan = keep.tile([P, W], F32, name="pan%d" % t)
            pb = keep.tile([P, W], F32, name="pb%d" % t)
            nc.vector.tensor_scalar(pan[:], s[:].indirect(l_n4[:]), -1.0, 0.0, ALU.mult, ALU.add)
            nc.vector.tensor_copy(pb[:], s[:].indirect(l_n5[:]))
            staged = keep.tile([P, W], F32, name="staged%d" % t, tag="staged%d" % t)
            nc.scalar.activation(staged[:], turn_sum([pb[:], pan[:]], W, "duel", 2)[:], ACT.Tanh, scale=0.5)
            th = turn_sum([staged[:]], W, "gap", 3)
            sb = keep.tile([P, W], F32, name="sb%d" % t)
            nc.scalar.activation(sb[:], th[:], ACT.Copy, scale=0.5, bias=0.5)
            duel.append((pan, th, pb, sb))
        for pair in ((0, 1), (2, 3)):
            res = {}
            for t in pair:
                pan, th, pb, sb = duel[t]
                res[t] = keep.tile([P, S], F32, name="res%d" % t, tag="s%d" % (PACK - 1 - t))
                nc.vector.tensor_tensor(res[t][:].indirect(l_n5[:]), pb[:], sb[:], ALU.mult)
            for t in pair:
                pan, th, pb, sb = duel[t]
                san = keep.tile([P, W], F32, name="san%d" % t, tag="staged%d" % (pair[1] + pair[0] - t))
                nc.scalar.activation(san[:], sb[:], ACT.Copy, bias=-1.0)
                nc.vector.tensor_tensor(res[t][:].indirect(l_n4[:]), pan[:], san[:], ALU.mult)
                nc.sync.dma_start(out_t[t], res[t][:])
